import numpy as np
import ml_dtypes


def mxq(x, axis, fmt="e4m3"):
    dtype, down = {"e4m3": (ml_dtypes.float8_e4m3fn, 7), "e5m2": (ml_dtypes.float8_e5m2, 14)}[fmt]
    v = np.moveaxis(np.asarray(x, np.float32).astype(ml_dtypes.bfloat16).astype(np.float64), axis, -1)
    blocks = v.reshape(v.shape[:-1] + (-1, 32))
    amax = np.abs(blocks).max(-1, keepdims=True)
    byte = np.maximum(np.where(amax > 0, np.frexp(amax)[1] - 1 + 127, 0) - down, 1)
    scale = np.exp2(byte - 127.0)
    codes = (blocks / scale).astype(np.float32).astype(dtype).astype(np.float64)
    return np.moveaxis((codes * scale).reshape(v.shape), -1, axis)


WIDE = False


def mx_kscale(k):
    if not WIDE:
        return np.ones(k)
    levels = np.array([30, -30])
    if k % 512:
        return np.exp2(np.random.permutation(np.resize(levels, k // 32))).repeat(32)
    a = np.empty((k // 512, 16))
    for p in range(k // 512):
        a[p, :8] = np.random.permutation(np.resize(levels, 8))
        for g in range(8):
            far = levels[np.abs(levels - a[p, g]) >= 10]
            a[p, g + 8] = far[np.random.randint(len(far))]
    return np.exp2(a.ravel()).repeat(32)


def f64(x):
    return np.asarray(x).astype(np.float64)


def striped(idx):
    return np.tile(np.asarray(idx).reshape(-1, 16).T, (8, 1)).astype(np.uint16)


def unstriped(offs):
    return offs[:16].T.reshape(-1).astype(np.int64)


E2M1 = np.array([0.0, 0.5, 1.0, 1.5, 2.0, 3.0, 4.0, 6.0, -0.0, -0.5, -1.0, -1.5, -2.0, -3.0, -4.0, -6.0])


def pack_weight(w, fmt):
    k, n = w.shape
    w = f64(np.asarray(w, np.float32).astype(ml_dtypes.bfloat16)).reshape(k // 32, 32, n)
    amax = np.abs(w).max(1)
    if fmt == "e4m3":
        byte = np.frexp(amax)[1] - 1 + 127 - 7
    else:
        mant, ex = np.frexp(amax / 6.0)
        byte = np.where(mant > 0.5, ex, ex - 1) + 127
    byte = np.clip(np.where(amax > 0, byte, 1), 1, 254)
    scaled = (w * np.exp2(127.0 - byte)[:, None, :]).reshape(k, n).astype(np.float32)
    by_word = np.ascontiguousarray(scaled.reshape(k // 512, 128, 4, n).transpose(0, 1, 3, 2))
    if fmt == "e4m3":
        words = by_word.astype(ml_dtypes.float8_e4m3fn).view(np.uint8)
    else:
        c = by_word.astype(ml_dtypes.float4_e2m1fn).view(np.uint8) & 0xF
        words = (c[..., 0::2] | (c[..., 1::2] << 4)).reshape(k // 512, 128, 2 * n)
    return np.ascontiguousarray(words), np.ascontiguousarray(byte.astype(np.uint8).reshape(k // 512, 16, n))


def unpack_weight(words, scales, fmt):
    g, _, n = scales.shape
    words = np.ascontiguousarray(words).reshape(g, 128, n, -1)
    if fmt == "e4m3":
        vals = words.view(ml_dtypes.float8_e4m3fn).astype(np.float64)
    else:
        nib = np.empty((g, 128, n, 4), np.uint8)
        nib[..., 0::2] = words & 0xF
        nib[..., 1::2] = words >> 4
        vals = E2M1[nib]
    vals = vals * np.repeat(np.exp2(scales.astype(np.float64) - 127.0), 8, axis=1)[..., None]
    return vals.transpose(0, 1, 3, 2).reshape(g * 512, n)


def bf(x):
    return np.asarray(x, np.float32).astype(ml_dtypes.bfloat16)


def planes(Y):
    r, m = Y.shape
    b = f64(bf(Y)).reshape(r // 32, 32, m)
    amax = np.abs(b).max(1)
    byte = np.clip(np.where(amax > 0, np.frexp(amax)[1] - 1 + 127 - 7, 1), 1, 254)
    codes = (b * np.exp2(127.0 - byte)[:, None, :]).reshape(r, m).astype(np.float32).astype(ml_dtypes.float8_e4m3fn).view(np.uint8)
    words = codes.reshape(r // 512, 128, 4, m).transpose(0, 1, 3, 2)
    return np.ascontiguousarray(words), np.ascontiguousarray(byte.astype(np.uint8).reshape(r // 512, 16, m))


K, T, J, I, L, S, R, V, N = 512, 1024, 256, 128, 128, 512, 512, 512, 512


def setup_inputs():
    n = np.random.standard_normal
    idx = np.random.permutation(T)[:I]
    idx2 = np.random.permutation(S)[:L]
    idx3 = np.random.permutation(V)[:J]
    fk = mx_kscale(K)
    fr = mx_kscale(R)
    wp = pack_weight(n((K, R)) * 1 / np.sqrt(K) * fk[:, None] * fr, "e4m3")
    wbp = pack_weight(n((R, N)) * 1 / np.sqrt(R) / fr[:, None], "e2m1")
    return {
        "xa": (n((K, T)) / fk[:, None]).astype(np.float32),
        "xb": (n((K, S)) * 0.6 / fk[:, None]).astype(np.float32),
        "w_words": wp[0],
        "w_scales": wp[1],
        "tb": (n((R, V)) * 0.7 * fr[:, None]).astype(np.float32),
        "wb_words": wbp[0],
        "wb_scales": wbp[1],
        "rs": (n((N, J))).astype(np.float32),
        "gm": (np.random.uniform(0.5, 2.0, (N, 1))).astype(np.float32),
        "offs": striped(idx),
        "offs2": striped(idx2),
        "offs3": striped(idx3),
    }


def reference(xa, xb, w_words, w_scales, tb, wb_words, wb_scales, rs, gm, offs, offs2, offs3):
    idx = unstriped(offs)
    idx2 = unstriped(offs2)
    idx3 = unstriped(offs3)
    wu = unpack_weight(w_words, w_scales, "e4m3")
    wbu = unpack_weight(wb_words, wb_scales, "e2m1")
    u = np.concatenate([f64(xa)[:, idx], f64(xb)[:, idx2]], axis=1)
    uq = mxq(u, 0, "e4m3")
    a = wu.T @ uq
    hid = np.maximum(a - f64(tb)[:, idx3], 0.0)
    hidq = mxq(hid, 0, "e5m2")
    p = wbu.T @ hidq
    y = f64(gm) * p + f64(rs)
    words, scales = planes(y)
    return y, words, scales

@@ -1,0 +1,167 @@
+from contextlib import ExitStack
+
+import concourse.mybir as mybir
+
+K, T, J, S, R, V, N = 512, 1024, 256, 512, 512, 512, 512
+FLOPS = 2 * K * R * J + 2 * R * N * J
+
+F32 = mybir.dt.float32
+BF16 = mybir.dt.bfloat16
+I32 = mybir.dt.int32
+U32 = mybir.dt.uint32
+U16 = mybir.dt.uint16
+U8 = mybir.dt.uint8
+E4M3 = mybir.dt.float8_e4m3fn_x4
+E5M2 = mybir.dt.float8_e5m2_x4
+E2M1 = mybir.dt.float4_e2m1fn_x4
+ALU = mybir.AluOpType
+COPY = mybir.ActivationFunctionType.Copy
+
+P = 128
+PACK = 4
+HALF = J // 2
+QUADS = 4
+
+
+def tile_list_joined_overtable_residual_pl_kernel(
+    tc, xa, xb, w_words, w_scales, tb, wb_words, wb_scales, rs, gm, offs, offs2, offs3, out_0, out_1, out_2
+):
+    nc = tc.nc
+    with ExitStack() as ctx:
+        sb = ctx.enter_context(tc.tile_pool(name="sb", bufs=1))
+        ps = ctx.enter_context(tc.psum_pool(name="ps", bufs=1))
+
+        def rows(x):
+            return x.rearrange("(p t) c -> p t c", t=PACK)
+
+        ws_raw = sb.tile([P, R], U8, name="ws_raw")
+        wbs_raw = sb.tile([P, N], U8, name="wbs_raw")
+        for raw, src in ((ws_raw, w_scales), (wbs_raw, wb_scales)):
+            nc.gpsimd.memset(raw[:].bitcast(I32), 0)
+            for q in range(QUADS):
+                nc.gpsimd.dma_start(raw[32 * q : 32 * q + 4, :].bitcast(I32), src[0, 4 * q : 4 * q + 4, :].bitcast(I32))
+
+        tb_sb = sb.tile([P, PACK, V], F32, name="tb_sb")
+        nc.sync.dma_start(tb_sb[:], rows(tb))
+        list_tb = sb.tile([P, J // 16], U16, name="list_tb")
+        nc.sync.dma_start(list_tb[:], offs3)
+        w_raw = sb.tile([P, R], U32, name="w_raw")
+        nc.sync.dma_start(w_raw[:].bitcast(I32), w_words[0].rearrange("p c r -> p (c r)").bitcast(I32))
+        wb_raw = sb.tile([P, 2 * N], U8, name="wb_raw")
+        nc.sync.dma_start(wb_raw[:].bitcast(I32), wb_words[0].bitcast(I32))
+        list_b = sb.tile([P, HALF // 16], U16, name="list_b")
+        nc.sync.dma_start(list_b[:], offs2)
+        xb_sb = []
+        for h in range(2):
+            xt = sb.tile([P, 2, S], F32, name=f"xb{h}")
+            nc.sync.dma_start(xt[:], rows(xb)[:, 2 * h : 2 * h + 2, :])
+            xb_sb.extend([xt[:, 0, :], xt[:, 1, :]])
+        list_a = sb.tile([P, HALF // 16], U16, name="list_a")
+        nc.sync.dma_start(list_a[:], offs)
+        gm_sb = sb.tile([P, PACK], F32, name="gm_sb")
+        nc.sync.dma_start(gm_sb[:], gm.rearrange("(p t) o -> p (t o)", t=PACK))
+        xa_sb = []
+        for t in range(PACK):
+            xt = sb.tile([P, T], F32, name=f"xa{t}")
+            nc.sync.dma_start(xt[:], rows(xa)[:, t, :])
+            xa_sb.append(xt[:])
+        rs_sb = {}
+        for h in (1, 0):
+            rs_sb[h] = sb.tile([P, PACK, HALF], F32, name=f"rs{h}")
+            nc.sync.dma_start(rs_sb[h][:], rows(rs)[:, :, h * HALF : (h + 1) * HALF])
+
+        tb_g = sb.tile([P, PACK, J], F32, name="tb_g")
+        for t in range(PACK):
+            nc.scalar.activation(tb_g[:, t, :], tb_sb[:, t, :].indirect(list_tb[:]), COPY)
+        tb_i = {}
+        for h in (1, 0):
+            tb_i[h] = sb.tile([P, HALF, PACK], F32, name=f"tb_i{h}")
+            nc.scalar.copy(tb_i[h][:], tb_g[:, :, h * HALF : (h + 1) * HALF].rearrange("p t j -> p j t"))
+
+        def deal(dst, src, line):
+            nc.vector.tensor_copy(
+                dst.rearrange("p (t b i) -> p b t i", t=PACK, i=line),
+                src.rearrange("p (b i t) -> p b t i", t=PACK, i=line),
+            )
+
+        w_sb = sb.tile([P, R], U32, name="w_sb", align_bytes=64)
+        wb_sb = sb.tile([P, 2 * N], U8, name="wb_sb", align_bytes=64)
+        ws_sb = sb.tile([P, R], U8, name="ws_sb", align_bytes=64)
+        wbs_sb = sb.tile([P, N], U8, name="wbs_sb", align_bytes=64)
+        deal(w_sb[:], w_raw[:], 4)
+        deal(wb_sb[:].bitcast(U16), wb_raw[:].bitcast(U16), 8)
+        deal(ws_sb[:], ws_raw[:], 16)
+
+        def quantise(name, src, fmt):
+            codes = sb.tile([P, HALF], U32, name=f"{name}_codes", align_bytes=64)
+            scales = sb.tile([P, HALF], U8, name=f"{name}_scales", align_bytes=64)
+            nc.vector.quantize_mx(out=codes[:].bitcast(fmt), scales=scales[:], in_=src[:].rearrange("p j t -> p (j t)"))
+            return codes, scales
+
+        def first_stage(h, planes, picks):
+            u = sb.tile([P, HALF, PACK], BF16, name=f"u{h}", align_bytes=64)
+            for t in range(PACK):
+                nc.vector.tensor_copy(u[:, :, t], planes[t].indirect(picks[:]))
+            codes, scales = quantise(f"u{h}", u, E4M3)
+            a = ps.tile([P, PACK, HALF], F32, name=f"a{h}")
+            for t in range(PACK):
+                cols = slice(t * P, (t + 1) * P)
+                nc.tensor.matmul_mx(
+                    out=a[:, t, :], lhsT=w_sb[:, cols].bitcast(E4M3), lhsT_scale=ws_sb[:, cols],
+                    rhs=codes[:].bitcast(E4M3), rhs_scale=scales[:], start=True, stop=True,
+                )
+            return a
+
+        def second_stage(h, a, outs):
+            hid = sb.tile([P, HALF, PACK], BF16, name=f"hid{h}", align_bytes=64)
+            nc.vector.tensor_tensor(hid[:], a[:].rearrange("p t j -> p j t"), tb_i[h][:], ALU.subtract)
+            flat = hid[:].rearrange("p j t -> p (j t)")
+            nc.vector.tensor_scalar(flat, flat, 0.0, None, ALU.max)
+            codes, scales = quantise(f"hid{h}", hid, E5M2)
+            for t in range(PACK):
+                nc.tensor.matmul_mx(
+                    out=outs[t], lhsT=wb_sb[:, 2 * t * P : 2 * (t + 1) * P].bitcast(E2M1),
+                    lhsT_scale=wbs_sb[:, t * P : (t + 1) * P],
+                    rhs=codes[:].bitcast(E5M2), rhs_scale=scales[:], start=True, stop=True,
+                )
+
+        y_bf = sb.tile([P, J, PACK], BF16, name="y_bf", align_bytes=64)
+        y_codes = sb.tile([P, J], U32, name="y_codes", align_bytes=64)
+        y_scales = sb.tile([P, J], U8, name="y_scales", align_bytes=64)
+        words_out = out_1[0].rearrange("p c r -> p (c r)").bitcast(I32)
+
+        def planes_of(h):
+            cols = slice(h * HALF, (h + 1) * HALF)
+            nc.vector.quantize_mx(
+                out=y_codes[:, cols].bitcast(E4M3), scales=y_scales[:, cols],
+                in_=y_bf[:, cols, :].rearrange("p j t -> p (j t)"),
+            )
+            nc.sync.dma_start(words_out[:, cols], y_codes[:, cols].bitcast(I32))
+
+        a1 = first_stage(1, xb_sb, list_b)
+        deal(wbs_sb[:], wbs_raw[:], 16)
+        p1 = ps.tile([P, PACK, HALF], F32, name="p1")
+        second_stage(1, a1, [p1[:, t, :] for t in range(PACK)])
+        gp1 = sb.tile([P, PACK, HALF], F32, name="gp1")
+        for t in range(PACK):
+            nc.scalar.activation(gp1[:, t, :], p1[:, t, :], COPY, scale=gm_sb[:, t : t + 1])
+
+        a0 = first_stage(0, xa_sb, list_a)
+        y1 = sb.tile([P, PACK, HALF], F32, name="y1")
+        nc.vector.tensor_tensor(y1[:], gp1[:], rs_sb[1][:], ALU.add)
+        nc.sync.dma_start(rows(out_0)[:, :, HALF:], y1[:])
+        nc.scalar.copy(y_bf[:, HALF:, :], y1[:].rearrange("p t j -> p j t"))
+        p0 = [ps.tile([P, HALF], F32, name=f"p0_{t}") for t in range(PACK)]
+        second_stage(0, a0, [p0[t][:] for t in range(PACK)])
+        planes_of(1)
+        y0 = sb.tile([P, PACK, HALF], F32, name="y0")
+        for t in range(PACK):
+            nc.vector.scalar_tensor_tensor(
+                y0[:, t, :], p0[t][:], gm_sb[:, t : t + 1], rs_sb[0][:, t, :], ALU.mult, ALU.add
+            )
+        nc.sync.dma_start(rows(out_0)[:, :, :HALF], y0[:])
+        nc.vector.tensor_copy(y_bf[:, :HALF, :], y0[:].rearrange("p t j -> p j t"))
+        planes_of(0)
+        for q in range(QUADS):
+            queue = nc.scalar if q < 2 else nc.sync
+            queue.dma_start(out_2[0, 4 * q : 4 * q + 4, :].bitcast(I32), y_scales[32 * q : 32 * q + 4, :].bitcast(I32))

@@ -35,48 +35,58 @@ def tile_list_joined_overtable_residual_pl_kernel(
             return x.rearrange("(p t) c -> p t c", t=PACK)
 
         ws_raw = sb.tile([P, R], U8, name="ws_raw")
-        wbs_raw = sb.tile([P, N], U8, name="wbs_raw")
-        for raw, src in ((ws_raw, w_scales), (wbs_raw, wb_scales)):
-            nc.gpsimd.memset(raw[:].bitcast(I32), 0)
-            for q in range(QUADS):
-                nc.gpsimd.dma_start(raw[32 * q : 32 * q + 4, :].bitcast(I32), src[0, 4 * q : 4 * q + 4, :].bitcast(I32))
+        wbs_raw = sb.tile([P, N], U8, name="wbs_raw", tag="hid1_codes", align_bytes=64)
+        nc.vector.memset(ws_raw[:].bitcast(I32), 0)
+        nc.vector.memset(wbs_raw[:].bitcast(I32), 0)
 
-        tb_sb = sb.tile([P, PACK, V], F32, name="tb_sb")
-        nc.sync.dma_start(tb_sb[:], rows(tb))
-        list_tb = sb.tile([P, J // 16], U16, name="list_tb")
-        nc.sync.dma_start(list_tb[:], offs3)
+        def load_scales(raw, src, q):
+            nc.sync.dma_start(raw[32 * q : 32 * q + 4, :].bitcast(I32), src[0, 4 * q : 4 * q + 4, :].bitcast(I32))
+
+        def load_planes(name, x, first, count):
+            xt = sb.tile([P, count, x.shape[1]], F32, name=name)
+            nc.sync.dma_start(xt[:], rows(x)[:, first : first + count, :])
+            return [xt[:, i, :] for i in range(count)]
+
+        def load_list(name, src):
+            lt = sb.tile([P, src.shape[1]], U16, name=name)
+            nc.sync.dma_start(lt[:], src)
+            return lt
+
+        tb_sb = load_planes("tb01", tb, 0, 2)
+        list_tb = load_list("list_tb", offs3)
+        load_scales(ws_raw, w_scales, 0)
+        xb_sb = load_planes("xb01", xb, 0, 2)
+        list_b = load_list("list_b", offs2)
+        load_scales(ws_raw, w_scales, 1)
+        xb_sb = xb_sb + load_planes("xb23", xb, 2, 2)
+        load_scales(ws_raw, w_scales, 2)
+        load_scales(ws_raw, w_scales, 3)
         w_raw = sb.tile([P, R], U32, name="w_raw")
         nc.sync.dma_start(w_raw[:].bitcast(I32), w_words[0].rearrange("p c r -> p (c r)").bitcast(I32))
         wb_raw = sb.tile([P, 2 * N], U8, name="wb_raw")
         nc.sync.dma_start(wb_raw[:].bitcast(I32), wb_words[0].bitcast(I32))
-        list_b = sb.tile([P, HALF // 16], U16, name="list_b")
-        nc.sync.dma_start(list_b[:], offs2)
-        xb_sb = []
-        for h in range(2):
-            xt = sb.tile([P, 2, S], F32, name=f"xb{h}")
-            nc.sync.dma_start(xt[:], rows(xb)[:, 2 * h : 2 * h + 2, :])
-            xb_sb.extend([xt[:, 0, :], xt[:, 1, :]])
-        list_a = sb.tile([P, HALF // 16], U16, name="list_a")
-        nc.sync.dma_start(list_a[:], offs)
+        tb_sb = tb_sb + load_planes("tb23", tb, 2, 2)
+        for q in range(QUADS):
+            load_scales(wbs_raw, wb_scales, q)
+        xa_sb = load_planes("xa0", xa, 0, 1)
+        list_a = load_list("list_a", offs)
+        xa_sb = xa_sb + load_planes("xa1", xa, 1, 1)
         gm_sb = sb.tile([P, PACK], F32, name="gm_sb")
         nc.sync.dma_start(gm_sb[:], gm.rearrange("(p t) o -> p (t o)", t=PACK))
-        xa_sb = []
-        for t in range(PACK):
-            xt = sb.tile([P, T], F32, name=f"xa{t}")
-            nc.sync.dma_start(xt[:], rows(xa)[:, t, :])
-            xa_sb.append(xt[:])
+        xa_sb = xa_sb + load_planes("xa2", xa, 2, 1) + load_planes("xa3", xa, 3, 1)
         rs_sb = {}
         for h in (1, 0):
             rs_sb[h] = sb.tile([P, PACK, HALF], F32, name=f"rs{h}")
             nc.sync.dma_start(rs_sb[h][:], rows(rs)[:, :, h * HALF : (h + 1) * HALF])
 
-        tb_g = sb.tile([P, PACK, J], F32, name="tb_g")
-        for t in range(PACK):
-            nc.scalar.activation(tb_g[:, t, :], tb_sb[:, t, :].indirect(list_tb[:]), COPY)
-        tb_i = {}
-        for h in (1, 0):
-            tb_i[h] = sb.tile([P, HALF, PACK], F32, name=f"tb_i{h}")
-            nc.scalar.copy(tb_i[h][:], tb_g[:, :, h * HALF : (h + 1) * HALF].rearrange("p t j -> p j t"))
+        tb_g = {h: sb.tile([P, PACK, HALF], F32, name=f"tb_g{h}") for h in (1, 0)}
+        for pair in range(2):
+            for h in (1, 0):
+                for t in (2 * pair, 2 * pair + 1):
+                    picks = list_tb[:, h * HALF // 16 : (h + 1) * HALF // 16]
+                    nc.scalar.activation(tb_g[h][:, t, :], tb_sb[t].indirect(picks), COPY)
+        tb_i0 = sb.tile([P, HALF, PACK], F32, name="tb_i0")
+        nc.scalar.copy(tb_i0[:], tb_g[0][:].rearrange("p t j -> p j t"))
 
         def deal(dst, src, line):
             nc.vector.tensor_copy(
@@ -89,18 +99,24 @@ def tile_list_joined_overtable_residual_pl_kernel(
         ws_sb = sb.tile([P, R], U8, name="ws_sb", align_bytes=64)
         wbs_sb = sb.tile([P, N], U8, name="wbs_sb", align_bytes=64)
         deal(w_sb[:], w_raw[:], 4)
-        deal(wb_sb[:].bitcast(U16), wb_raw[:].bitcast(U16), 8)
         deal(ws_sb[:], ws_raw[:], 16)
 
         def quantise(name, src, fmt):
-            codes = sb.tile([P, HALF], U32, name=f"{name}_codes", align_bytes=64)
+            codes = sb.tile([P, HALF], U32, name=f"{name}_codes", tag=f"{name}_codes", align_bytes=64)
             scales = sb.tile([P, HALF], U8, name=f"{name}_scales", align_bytes=64)
             nc.vector.quantize_mx(out=codes[:].bitcast(fmt), scales=scales[:], in_=src[:].rearrange("p j t -> p (j t)"))
             return codes, scales
 
         def first_stage(h, planes, picks):
-            u = sb.tile([P, HALF, PACK], BF16, name=f"u{h}", align_bytes=64)
-            for t in range(PACK):
+            u = sb.tile([P, HALF, PACK], BF16, name=f"u{h}", tag="reused" if h == 0 else "u1", align_bytes=64)
+            first = 0
+            if h == 0:
+                first = 2
+                early = sb.tile([P, first, HALF], BF16, name="early")
+                for t in range(first):
+                    nc.scalar.activation(early[:, t, :], planes[t].indirect(picks[:]), COPY)
+                nc.vector.tensor_copy(u[:, :, :first], early[:].rearrange("p t j -> p j t"))
+            for t in range(first, PACK):
                 nc.vector.tensor_copy(u[:, :, t], planes[t].indirect(picks[:]))
             codes, scales = quantise(f"u{h}", u, E4M3)
             a = ps.tile([P, PACK, HALF], F32, name=f"a{h}")
@@ -113,10 +129,15 @@ def tile_list_joined_overtable_residual_pl_kernel(
             return a
 
         def second_stage(h, a, outs):
-            hid = sb.tile([P, HALF, PACK], BF16, name=f"hid{h}", align_bytes=64)
-            nc.vector.tensor_tensor(hid[:], a[:].rearrange("p t j -> p j t"), tb_i[h][:], ALU.subtract)
-            flat = hid[:].rearrange("p j t -> p (j t)")
-            nc.vector.tensor_scalar(flat, flat, 0.0, None, ALU.max)
+            hid = sb.tile([P, HALF, PACK], BF16, name=f"hid{h}", tag="reused" if h == 1 else "hid0", align_bytes=64)
+            if h == 1:
+                diff = sb.tile([P, PACK, HALF], BF16, name="diff")
+                nc.vector.tensor_tensor(diff[:], a[:], tb_g[1][:], ALU.subtract)
+                nc.vector.tensor_scalar(hid[:], diff[:].rearrange("p t j -> p j t"), 0.0, None, ALU.max)
+            else:
+                nc.vector.tensor_tensor(hid[:], a[:].rearrange("p t j -> p j t"), tb_i0[:], ALU.subtract)
+                flat = hid[:].rearrange("p j t -> p (j t)")
+                nc.vector.tensor_scalar(flat, flat, 0.0, None, ALU.max)
             codes, scales = quantise(f"hid{h}", hid, E5M2)
             for t in range(PACK):
                 nc.tensor.matmul_mx(
@@ -139,6 +160,7 @@ def tile_list_joined_overtable_residual_pl_kernel(
             nc.sync.dma_start(words_out[:, cols], y_codes[:, cols].bitcast(I32))
 
         a1 = first_stage(1, xb_sb, list_b)
+        deal(wb_sb[:].bitcast(U16), wb_raw[:].bitcast(U16), 8)
         deal(wbs_sb[:], wbs_raw[:], 16)
         p1 = ps.tile([P, PACK, HALF], F32, name="p1")
         second_stage(1, a1, [p1[:, t, :] for t in range(PACK)])
@@ -147,7 +169,7 @@ def tile_list_joined_overtable_residual_pl_kernel(
             nc.scalar.activation(gp1[:, t, :], p1[:, t, :], COPY, scale=gm_sb[:, t : t + 1])
 
         a0 = first_stage(0, xa_sb, list_a)
-        y1 = sb.tile([P, PACK, HALF], F32, name="y1")
+        y1 = sb.tile([P, PACK, HALF], F32, name="y1", tag="reused", align_bytes=64)
         nc.vector.tensor_tensor(y1[:], gp1[:], rs_sb[1][:], ALU.add)
         nc.sync.dma_start(rows(out_0)[:, :, HALF:], y1[:])
         nc.scalar.copy(y_bf[:, HALF:, :], y1[:].rearrange("p t j -> p j t"))

from contextlib import ExitStack

import concourse.mybir as mybir

K, T, J, S, R, V, N = 512, 1024, 256, 512, 512, 512, 512
FLOPS = 2 * K * R * J + 2 * R * N * J

F32 = mybir.dt.float32
BF16 = mybir.dt.bfloat16
I32 = mybir.dt.int32
U32 = mybir.dt.uint32
U16 = mybir.dt.uint16
U8 = mybir.dt.uint8
E4M3 = mybir.dt.float8_e4m3fn_x4
E5M2 = mybir.dt.float8_e5m2_x4
E2M1 = mybir.dt.float4_e2m1fn_x4
ALU = mybir.AluOpType
COPY = mybir.ActivationFunctionType.Copy

P = 128
PACK = 4
HALF = J // 2
QUADS = 4


def tile_list_joined_overtable_residual_pl_kernel(
    tc, xa, xb, w_words, w_scales, tb, wb_words, wb_scales, rs, gm, offs, offs2, offs3, out_0, out_1, out_2
):
    nc = tc.nc
    with ExitStack() as ctx:
        sb = ctx.enter_context(tc.tile_pool(name="sb", bufs=1))
        ps = ctx.enter_context(tc.psum_pool(name="ps", bufs=1))

        def rows(x):
            return x.rearrange("(p t) c -> p t c", t=PACK)

        ws_raw = sb.tile([P, R], U8, name="ws_raw")
        wbs_raw = sb.tile([P, N], U8, name="wbs_raw", tag="hid1_codes", align_bytes=64)
        nc.vector.memset(ws_raw[:].bitcast(I32), 0)
        nc.vector.memset(wbs_raw[:].bitcast(I32), 0)

        def load_scales(raw, src, q):
            nc.sync.dma_start(raw[32 * q : 32 * q + 4, :].bitcast(I32), src[0, 4 * q : 4 * q + 4, :].bitcast(I32))

        def load_planes(name, x, first, count):
            xt = sb.tile([P, count, x.shape[1]], F32, name=name)
            nc.sync.dma_start(xt[:], rows(x)[:, first : first + count, :])
            return [xt[:, i, :] for i in range(count)]

        def load_list(name, src):
            lt = sb.tile([P, src.shape[1]], U16, name=name)
            nc.sync.dma_start(lt[:], src)
            return lt

        tb_sb = load_planes("tb01", tb, 0, 2)
        list_tb = load_list("list_tb", offs3)
        load_scales(ws_raw, w_scales, 0)
        xb_sb = load_planes("xb01", xb, 0, 2)
        list_b = load_list("list_b", offs2)
        load_scales(ws_raw, w_scales, 1)
        xb_sb = xb_sb + load_planes("xb23", xb, 2, 2)
        load_scales(ws_raw, w_scales, 2)
        load_scales(ws_raw, w_scales, 3)
        w_raw = sb.tile([P, R], U32, name="w_raw")
        nc.sync.dma_start(w_raw[:].bitcast(I32), w_words[0].rearrange("p c r -> p (c r)").bitcast(I32))
        wb_raw = sb.tile([P, 2 * N], U8, name="wb_raw")
        nc.sync.dma_start(wb_raw[:].bitcast(I32), wb_words[0].bitcast(I32))
        tb_sb = tb_sb + load_planes("tb23", tb, 2, 2)
        for q in range(QUADS):
            load_scales(wbs_raw, wb_scales, q)
        xa_sb = load_planes("xa0", xa, 0, 1)
        list_a = load_list("list_a", offs)
        xa_sb = xa_sb + load_planes("xa1", xa, 1, 1)
        gm_sb = sb.tile([P, PACK], F32, name="gm_sb")
        nc.sync.dma_start(gm_sb[:], gm.rearrange("(p t) o -> p (t o)", t=PACK))
        xa_sb = xa_sb + load_planes("xa2", xa, 2, 1) + load_planes("xa3", xa, 3, 1)
        rs_sb = {}
        for h in (1, 0):
            rs_sb[h] = sb.tile([P, PACK, HALF], F32, name=f"rs{h}")
            nc.sync.dma_start(rs_sb[h][:], rows(rs)[:, :, h * HALF : (h + 1) * HALF])

        tb_g = {h: sb.tile([P, PACK, HALF], F32, name=f"tb_g{h}") for h in (1, 0)}
        for pair in range(2):
            for h in (1, 0):
                for t in (2 * pair, 2 * pair + 1):
                    picks = list_tb[:, h * HALF // 16 : (h + 1) * HALF // 16]
                    nc.scalar.activation(tb_g[h][:, t, :], tb_sb[t].indirect(picks), COPY)
        tb_i0 = sb.tile([P, HALF, PACK], F32, name="tb_i0")
        nc.scalar.copy(tb_i0[:], tb_g[0][:].rearrange("p t j -> p j t"))

        def deal(dst, src, line):
            nc.vector.tensor_copy(
                dst.rearrange("p (t b i) -> p b t i", t=PACK, i=line),
                src.rearrange("p (b i t) -> p b t i", t=PACK, i=line),
            )

        w_sb = sb.tile([P, R], U32, name="w_sb", align_bytes=64)
        wb_sb = sb.tile([P, 2 * N], U8, name="wb_sb", align_bytes=64)
        ws_sb = sb.tile([P, R], U8, name="ws_sb", align_bytes=64)
        wbs_sb = sb.tile([P, N], U8, name="wbs_sb", align_bytes=64)
        deal(w_sb[:], w_raw[:], 4)
        deal(ws_sb[:], ws_raw[:], 16)

        def quantise(name, src, fmt):
            codes = sb.tile([P, HALF], U32, name=f"{name}_codes", tag=f"{name}_codes", align_bytes=64)
            scales = sb.tile([P, HALF], U8, name=f"{name}_scales", align_bytes=64)
            nc.vector.quantize_mx(out=codes[:].bitcast(fmt), scales=scales[:], in_=src[:].rearrange("p j t -> p (j t)"))
            return codes, scales

        def first_stage(h, planes, picks):
            u = sb.tile([P, HALF, PACK], BF16, name=f"u{h}", tag="reused" if h == 0 else "u1", align_bytes=64)
            first = 0
            if h == 0:
                first = 2
                early = sb.tile([P, first, HALF], BF16, name="early")
                for t in range(first):
                    nc.scalar.activation(early[:, t, :], planes[t].indirect(picks[:]), COPY)
                nc.vector.tensor_copy(u[:, :, :first], early[:].rearrange("p t j -> p j t"))
            for t in range(first, PACK):
                nc.vector.tensor_copy(u[:, :, t], planes[t].indirect(picks[:]))
            codes, scales = quantise(f"u{h}", u, E4M3)
            a = ps.tile([P, PACK, HALF], F32, name=f"a{h}")
            for t in range(PACK):
                cols = slice(t * P, (t + 1) * P)
                nc.tensor.matmul_mx(
                    out=a[:, t, :], lhsT=w_sb[:, cols].bitcast(E4M3), lhsT_scale=ws_sb[:, cols],
                    rhs=codes[:].bitcast(E4M3), rhs_scale=scales[:], start=True, stop=True,
                )
            return a

        def second_stage(h, a, outs):
            hid = sb.tile([P, HALF, PACK], BF16, name=f"hid{h}", tag="reused" if h == 1 else "hid0", align_bytes=64)
            if h == 1:
                diff = sb.tile([P, PACK, HALF], BF16, name="diff")
                nc.vector.tensor_tensor(diff[:], a[:], tb_g[1][:], ALU.subtract)
                nc.vector.tensor_scalar(hid[:], diff[:].rearrange("p t j -> p j t"), 0.0, None, ALU.max)
            else:
                nc.vector.tensor_tensor(hid[:], a[:].rearrange("p t j -> p j t"), tb_i0[:], ALU.subtract)
                flat = hid[:].rearrange("p j t -> p (j t)")
                nc.vector.tensor_scalar(flat, flat, 0.0, None, ALU.max)
            codes, scales = quantise(f"hid{h}", hid, E5M2)
            for t in range(PACK):
                nc.tensor.matmul_mx(
                    out=outs[t], lhsT=wb_sb[:, 2 * t * P : 2 * (t + 1) * P].bitcast(E2M1),
                    lhsT_scale=wbs_sb[:, t * P : (t + 1) * P],
                    rhs=codes[:].bitcast(E5M2), rhs_scale=scales[:], start=True, stop=True,
                )

        y_bf = sb.tile([P, J, PACK], BF16, name="y_bf", align_bytes=64)
        y_codes = sb.tile([P, J], U32, name="y_codes", align_bytes=64)
        y_scales = sb.tile([P, J], U8, name="y_scales", align_bytes=64)
        words_out = out_1[0].rearrange("p c r -> p (c r)").bitcast(I32)

        def planes_of(h):
            cols = slice(h * HALF, (h + 1) * HALF)
            nc.vector.quantize_mx(
                out=y_codes[:, cols].bitcast(E4M3), scales=y_scales[:, cols],
                in_=y_bf[:, cols, :].rearrange("p j t -> p (j t)"),
            )
            nc.sync.dma_start(words_out[:, cols], y_codes[:, cols].bitcast(I32))

        a1 = first_stage(1, xb_sb, list_b)
        deal(wb_sb[:].bitcast(U16), wb_raw[:].bitcast(U16), 8)
        deal(wbs_sb[:], wbs_raw[:], 16)
        p1 = ps.tile([P, PACK, HALF], F32, name="p1")
        second_stage(1, a1, [p1[:, t, :] for t in range(PACK)])
        gp1 = sb.tile([P, PACK, HALF], F32, name="gp1")
        for t in range(PACK):
            nc.scalar.activation(gp1[:, t, :], p1[:, t, :], COPY, scale=gm_sb[:, t : t + 1])

        a0 = first_stage(0, xa_sb, list_a)
        y1 = sb.tile([P, PACK, HALF], F32, name="y1", tag="reused", align_bytes=64)
        nc.vector.tensor_tensor(y1[:], gp1[:], rs_sb[1][:], ALU.add)
        nc.sync.dma_start(rows(out_0)[:, :, HALF:], y1[:])
        nc.scalar.copy(y_bf[:, HALF:, :], y1[:].rearrange("p t j -> p j t"))
        p0 = [ps.tile([P, HALF], F32, name=f"p0_{t}") for t in range(PACK)]
        second_stage(0, a0, [p0[t][:] for t in range(PACK)])
        planes_of(1)
        y0 = sb.tile([P, PACK, HALF], F32, name="y0")
        for t in range(PACK):
            nc.vector.scalar_tensor_tensor(
                y0[:, t, :], p0[t][:], gm_sb[:, t : t + 1], rs_sb[0][:, t, :], ALU.mult, ALU.add
            )
        nc.sync.dma_start(rows(out_0)[:, :, :HALF], y0[:])
        nc.vector.tensor_copy(y_bf[:, :HALF, :], y0[:].rearrange("p t j -> p j t"))
        planes_of(0)
        for q in range(QUADS):
            queue = nc.scalar if q < 2 else nc.sync
            queue.dma_start(out_2[0, 4 * q : 4 * q + 4, :].bitcast(I32), y_scales[32 * q : 32 * q + 4, :].bitcast(I32))
